import numpy as np
import ml_dtypes


def mxq(x, axis, fmt="e4m3"):
    dtype, down = {"e4m3": (ml_dtypes.float8_e4m3fn, 7), "e5m2": (ml_dtypes.float8_e5m2, 14)}[fmt]
    v = np.moveaxis(np.asarray(x, np.float32).astype(ml_dtypes.bfloat16).astype(np.float64), axis, -1)
    blocks = v.reshape(v.shape[:-1] + (-1, 32))
    amax = np.abs(blocks).max(-1, keepdims=True)
    byte = np.maximum(np.where(amax > 0, np.frexp(amax)[1] - 1 + 127, 0) - down, 1)
    scale = np.exp2(byte - 127.0)
    codes = (blocks / scale).astype(np.float32).astype(dtype).astype(np.float64)
    return np.moveaxis((codes * scale).reshape(v.shape), -1, axis)


WIDE = False


def mx_kscale(k):
    if not WIDE:
        return np.ones(k)
    levels = np.array([10, -10, 5, -5, 0])
    if k % 512:
        return np.exp2(np.random.permutation(np.resize(levels, k // 32))).repeat(32)
    a = np.empty((k // 512, 16))
    for p in range(k // 512):
        a[p, :8] = np.random.permutation(np.resize(levels, 8))
        for g in range(8):
            far = levels[np.abs(levels - a[p, g]) >= 10]
            a[p, g + 8] = far[np.random.randint(len(far))]
    return np.exp2(a.ravel()).repeat(32)


def f64(x):
    return np.asarray(x).astype(np.float64)


def striped(idx):
    return np.tile(np.asarray(idx).reshape(-1, 16).T, (8, 1)).astype(np.uint16)


def unstriped(offs):
    return offs[:16].T.reshape(-1).astype(np.int64)


E2M1 = np.array([0.0, 0.5, 1.0, 1.5, 2.0, 3.0, 4.0, 6.0, -0.0, -0.5, -1.0, -1.5, -2.0, -3.0, -4.0, -6.0])


def pack_weight(w, fmt):
    k, n = w.shape
    w = f64(np.asarray(w, np.float32).astype(ml_dtypes.bfloat16)).reshape(k // 32, 32, n)
    amax = np.abs(w).max(1)
    if fmt == "e4m3":
        byte = np.frexp(amax)[1] - 1 + 127 - 7
    else:
        mant, ex = np.frexp(amax / 6.0)
        byte = np.where(mant > 0.5, ex, ex - 1) + 127
    byte = np.clip(np.where(amax > 0, byte, 1), 1, 254)
    scaled = (w * np.exp2(127.0 - byte)[:, None, :]).reshape(k, n).astype(np.float32)
    by_word = np.ascontiguousarray(scaled.reshape(k // 512, 128, 4, n).transpose(0, 1, 3, 2))
    if fmt == "e4m3":
        words = by_word.astype(ml_dtypes.float8_e4m3fn).view(np.uint8)
    else:
        c = by_word.astype(ml_dtypes.float4_e2m1fn).view(np.uint8) & 0xF
        words = (c[..., 0::2] | (c[..., 1::2] << 4)).reshape(k // 512, 128, 2 * n)
    return np.ascontiguousarray(words), np.ascontiguousarray(byte.astype(np.uint8).reshape(k // 512, 16, n))


def unpack_weight(words, scales, fmt):
    g, _, n = scales.shape
    words = np.ascontiguousarray(words).reshape(g, 128, n, -1)
    if fmt == "e4m3":
        vals = words.view(ml_dtypes.float8_e4m3fn).astype(np.float64)
    else:
        nib = np.empty((g, 128, n, 4), np.uint8)
        nib[..., 0::2] = words & 0xF
        nib[..., 1::2] = words >> 4
        vals = E2M1[nib]
    vals = vals * np.repeat(np.exp2(scales.astype(np.float64) - 127.0), 8, axis=1)[..., None]
    return vals.transpose(0, 1, 3, 2).reshape(g * 512, n)


def sigmoid(v):
    return 1.0 / (1.0 + np.exp(-v))


def sgn(shape):
    return np.random.uniform(0.5, 2.0, shape) * np.where(np.random.standard_normal(shape) < 0, -1.0, 1.0)


K, T, J, Q, R, O, N, E = 512, 1024, 256, 128, 512, 128, 256, 256


def setup_inputs():
    n = np.random.standard_normal
    idx = np.random.permutation(T)[:J]
    idx2 = np.random.permutation(J)[:O]
    idx3 = np.random.permutation(E)[:O]
    fk = mx_kscale(K)
    fr = mx_kscale(R)
    fr = fr / fr.max()
    xtp = pack_weight(n((K, T)) / fk[:, None], "e4m3")
    wp = pack_weight(n((K, Q)) * 1 / np.sqrt(K) * fk[:, None], "e2m1")
    wbp = pack_weight(n((R, N)) * 1 / np.sqrt(R) / fr[:, None], "e2m1")
    return {
        "xt_words": xtp[0],
        "xt_scales": xtp[1],
        "w_words": wp[0],
        "w_scales": wp[1],
        "sg": (0.35 * sgn((Q, 1))).astype(np.float32),
        "ba": (np.random.uniform(-3.2, -2.6, (Q, 1)) + np.log(fr[::4])[:, None]).astype(np.float32),
        "bb": (np.random.uniform(-2.5, -2.0, (Q, 1)) + np.log(fr[::4])[:, None]).astype(np.float32),
        "bc": (np.random.uniform(-1.9, -1.4, (Q, 1)) + np.log(fr[::4])[:, None]).astype(np.float32),
        "bd": (np.random.uniform(-1.3, -0.8, (Q, 1)) + np.log(fr[::4])[:, None]).astype(np.float32),
        "wb_words": wbp[0],
        "wb_scales": wbp[1],
        "so": (np.random.uniform(0.5, 1.6, (N, 1))).astype(np.float32),
        "offs": striped(idx),
        "offs2": striped(idx2),
        "offs3": striped(idx3),
    }


def reference(xt_words, xt_scales, w_words, w_scales, sg, ba, bb, bc, bd, wb_words, wb_scales, so, offs, offs2, offs3):
    idx = unstriped(offs)
    idx2 = unstriped(offs2)
    idx3 = unstriped(offs3)
    xtu = unpack_weight(xt_words, xt_scales, "e4m3")
    wu = unpack_weight(w_words, w_scales, "e2m1")
    wbu = unpack_weight(wb_words, wb_scales, "e2m1")
    xtidxg = xtu[:, idx]
    a = wu.T @ xtidxg
    v0 = sigmoid(a[:, idx2] * f64(sg) + f64(ba))
    v1 = sigmoid(a[:, idx2] * f64(sg) + f64(bb))
    v2 = sigmoid(a[:, idx2] * f64(sg) + f64(bc))
    v3 = sigmoid(a[:, idx2] * f64(sg) + f64(bd))
    hid = np.stack([v0, v1, v2, v3], axis=1).reshape(R, O)
    hidq = mxq(hid, 0, "e4m3")
    p = wbu.T @ hidq
    y = np.zeros((N, E))
    y[:, idx3] = p * f64(so)
    return y

@@ -1,0 +1,123 @@
+from contextlib import ExitStack
+
+import concourse.mybir as mybir
+
+F32 = mybir.dt.float32
+BF16 = mybir.dt.bfloat16
+I32 = mybir.dt.int32
+U32 = mybir.dt.uint32
+U16 = mybir.dt.uint16
+U8 = mybir.dt.uint8
+FP8X4 = mybir.dt.float8_e4m3fn_x4
+FP4X4 = mybir.dt.float4_e2m1fn_x4
+ACT = mybir.ActivationFunctionType
+
+K, T, J, Q, R, O, N, E = 512, 1024, 256, 128, 512, 128, 256, 256
+P = 128
+QUADS = 4
+FLOPS = 2 * K * Q * J + 2 * R * N * O
+
+
+def tile_list_thermometer_kernel(tc, xt_words, xt_scales, w_words, w_scales, sg, ba, bb, bc, bd,
+                                    wb_words, wb_scales, so, offs, offs2, offs3, out):
+    nc = tc.nc
+    with ExitStack() as ctx:
+        sb = ctx.enter_context(tc.tile_pool(name="sb", bufs=1))
+        ps = ctx.enter_context(tc.psum_pool(name="ps", bufs=1))
+        ctx.enter_context(nc.allow_non_contiguous_dma(reason="one float32 value a partition"))
+
+        xs_plane = sb.tile([P, T // 4], I32, name="xs_plane", align_bytes=64)
+        nc.vector.memset(xs_plane[:], 0)
+        ws_plane = sb.tile([P, Q // 4], I32, name="ws_plane", align_bytes=64)
+        nc.vector.memset(ws_plane[:], 0)
+        wbs_plane = sb.tile([P, N // 4], I32, name="wbs_plane", align_bytes=64)
+        nc.vector.memset(wbs_plane[:], 0)
+
+        ws_rows = sb.tile([4, QUADS, Q // 4], I32, name="ws_rows")
+        nc.scalar.dma_start(ws_rows[:], w_scales[0].bitcast(I32).rearrange("(q r) c -> r q c", r=4))
+        x_words = sb.tile([P, T], I32, name="x_words", align_bytes=64)
+        nc.scalar.dma_start(x_words[:], xt_words[0].rearrange("p c r -> p (c r)").bitcast(I32))
+
+        warm = sb.tile([P, 1], F32, name="warm")
+        nc.vector.memset(warm[:], 0.0)
+        warm_out = sb.tile([P, 1], F32, name="warm_out")
+        nc.scalar.activation(warm_out[:], warm[:], ACT.Sigmoid)
+
+        list1 = sb.tile([P, J // 16], U16, name="list1")
+        nc.sync.dma_start(list1[:], offs)
+        for q in range(QUADS):
+            nc.sync.dma_start(xs_plane[32 * q : 32 * q + 4, :], xt_scales[0].bitcast(I32)[4 * q : 4 * q + 4, :])
+        w_codes = sb.tile([P, Q // 2], I32, name="w_codes", align_bytes=64)
+        nc.sync.dma_start(w_codes[:], w_words[0].bitcast(I32))
+
+        list2 = sb.tile([P, O // 16], U16, name="list2")
+        nc.sync.dma_start(list2[:], offs2)
+        bias = [sb.tile([P, 1], F32, name="bias%d" % i) for i in range(4)]
+        for i, src in enumerate((ba, bb, bc, bd)):
+            nc.sync.dma_start(bias[i][:], src)
+        for q in range(QUADS):
+            nc.sync.dma_start(wbs_plane[32 * q : 32 * q + 4, :], wb_scales[0].bitcast(I32)[4 * q : 4 * q + 4, :])
+        list3 = sb.tile([P, O // 16], U16, name="list3")
+        nc.sync.dma_start(list3[:], offs3)
+
+        slope = sb.tile([P, 1], F32, name="slope")
+        nc.gpsimd.dma_start(slope[:], sg)
+        wb_codes = sb.tile([P, N // 2], I32, name="wb_codes", align_bytes=64)
+        nc.gpsimd.dma_start(wb_codes[:], wb_words[0].bitcast(I32))
+        gain = sb.tile([P, 2], F32, name="gain")
+        nc.gpsimd.dma_start(gain[:], so.rearrange("(h p) o -> p (h o)", p=P))
+
+        page = [sb.tile([P, E], F32, name="page%d" % h) for h in range(2)]
+        for h in range(2):
+            nc.vector.memset(page[h][:], 0.0)
+
+        for q in range(QUADS):
+            nc.vector.tensor_copy(ws_plane[32 * q : 32 * q + 4, :], ws_rows[:, q, :])
+
+        half = J // 2
+        g_scales = [sb.tile([P, half], U8, name="g_scales%d" % h, align_bytes=64) for h in range(2)]
+        g_words = [sb.tile([P, half], U32, name="g_words%d" % h, align_bytes=64) for h in range(2)]
+        part = [list1[:, h * (half // 16) : (h + 1) * (half // 16)] for h in range(2)]
+        for h in range(2):
+            nc.vector.tensor_copy(g_scales[h][:], xs_plane[:].bitcast(U8).indirect(part[h]))
+        a_sb = sb.tile([P, J], F32, name="a_sb")
+        a_ps = []
+        for h in range(2):
+            nc.vector.tensor_copy(g_words[h][:], x_words[:].bitcast(U32).indirect(part[h]))
+            acc = ps.tile([P, half], F32, name="a_ps%d" % h)
+            nc.tensor.matmul_mx(
+                out=acc[:],
+                lhsT=w_codes[:].bitcast(U8).bitcast(FP4X4),
+                lhsT_scale=ws_plane[:].bitcast(U8),
+                rhs=g_words[h][:].bitcast(FP8X4),
+                rhs_scale=g_scales[h][:],
+                start=True,
+                stop=True,
+            )
+            a_ps.append(acc)
+        nc.scalar.copy(a_sb[:, 0:half], a_ps[0][:])
+        nc.vector.tensor_copy(a_sb[:, half:J], a_ps[1][:])
+
+        hid = sb.tile([P, 4 * O], BF16, name="hid", align_bytes=64)
+        for i in range(4):
+            nc.scalar.activation(hid[:, i : 4 * O : 4], a_sb[:].indirect(list2[:]), ACT.Sigmoid, bias=bias[i][:], scale=slope[:])
+
+        h_codes = sb.tile([P, O], U32, name="h_codes", align_bytes=64)
+        h_scales = sb.tile([P, O], U8, name="h_scales", align_bytes=64)
+        nc.vector.quantize_mx(out=h_codes[:].bitcast(FP8X4), scales=h_scales[:], in_=hid[:])
+
+        for h in range(2):
+            p_ps = ps.tile([P, O], F32, name="p_ps%d" % h)
+            nc.tensor.matmul_mx(
+                out=p_ps[:],
+                lhsT=wb_codes[:].bitcast(U8)[:, 2 * P * h : 2 * P * (h + 1)].bitcast(FP4X4),
+                lhsT_scale=wbs_plane[:].bitcast(U8)[:, P * h : P * (h + 1)],
+                rhs=h_codes[:].bitcast(FP8X4),
+                rhs_scale=h_scales[:],
+                start=True,
+                stop=True,
+            )
+            p_sb = sb.tile([P, O], F32, name="p_sb%d" % h)
+            nc.vector.tensor_copy(p_sb[:], p_ps[:])
+            nc.scalar.activation(page[h][:].indirect(list3[:]), p_sb[:], ACT.Copy, scale=gain[:, h : h + 1])
+            nc.sync.dma_start(out[P * h : P * (h + 1), :], page[h][:])

@@ -15,6 +15,7 @@ ACT = mybir.ActivationFunctionType
 K, T, J, Q, R, O, N, E = 512, 1024, 256, 128, 512, 128, 256, 256
 P = 128
 QUADS = 4
+HEAD = 448
 FLOPS = 2 * K * Q * J + 2 * R * N * O
 
 
@@ -28,7 +29,7 @@ def tile_list_thermometer_kernel(tc, xt_words, xt_scales, w_words, w_scales, sg,
 
         xs_plane = sb.tile([P, T // 4], I32, name="xs_plane", align_bytes=64)
         nc.vector.memset(xs_plane[:], 0)
-        ws_plane = sb.tile([P, Q // 4], I32, name="ws_plane", align_bytes=64)
+        ws_plane = sb.tile([P, 2, Q // 4], I32, name="ws_plane", align_bytes=64)
         nc.vector.memset(ws_plane[:], 0)
         wbs_plane = sb.tile([P, N // 4], I32, name="wbs_plane", align_bytes=64)
         nc.vector.memset(wbs_plane[:], 0)
@@ -36,7 +37,10 @@ def tile_list_thermometer_kernel(tc, xt_words, xt_scales, w_words, w_scales, sg,
         ws_rows = sb.tile([4, QUADS, Q // 4], I32, name="ws_rows")
         nc.scalar.dma_start(ws_rows[:], w_scales[0].bitcast(I32).rearrange("(q r) c -> r q c", r=4))
         x_words = sb.tile([P, T], I32, name="x_words", align_bytes=64)
-        nc.scalar.dma_start(x_words[:], xt_words[0].rearrange("p c r -> p (c r)").bitcast(I32))
+        x_src = xt_words[0].rearrange("p c r -> p (c r)").bitcast(I32)
+        nc.scalar.dma_start(x_words[:, 0:HEAD], x_src[:, 0:HEAD])
+        for q in (2, 3):
+            nc.scalar.dma_start(xs_plane[32 * q : 32 * q + 4, :], xt_scales[0].bitcast(I32)[4 * q : 4 * q + 4, :])
 
         warm = sb.tile([P, 1], F32, name="warm")
         nc.vector.memset(warm[:], 0.0)
@@ -45,8 +49,9 @@ def tile_list_thermometer_kernel(tc, xt_words, xt_scales, w_words, w_scales, sg,
 
         list1 = sb.tile([P, J // 16], U16, name="list1")
         nc.sync.dma_start(list1[:], offs)
-        for q in range(QUADS):
+        for q in (0, 1):
             nc.sync.dma_start(xs_plane[32 * q : 32 * q + 4, :], xt_scales[0].bitcast(I32)[4 * q : 4 * q + 4, :])
+        nc.sync.dma_start(x_words[:, HEAD:T], x_src[:, HEAD:T])
         w_codes = sb.tile([P, Q // 2], I32, name="w_codes", align_bytes=64)
         nc.sync.dma_start(w_codes[:], w_words[0].bitcast(I32))
 
@@ -71,8 +76,9 @@ def tile_list_thermometer_kernel(tc, xt_words, xt_scales, w_words, w_scales, sg,
         for h in range(2):
             nc.vector.memset(page[h][:], 0.0)
 
-        for q in range(QUADS):
-            nc.vector.tensor_copy(ws_plane[32 * q : 32 * q + 4, :], ws_rows[:, q, :])
+        for q in range(2):
+            nc.vector.tensor_copy(ws_plane[32 * q : 32 * q + 4, :, :], ws_rows[:, q:QUADS:2, :])
+        nc.vector.tensor_copy(ws_plane[64:128, 0, :], ws_plane[0:64, 1, :])
 
         half = J // 2
         g_scales = [sb.tile([P, half], U8, name="g_scales%d" % h, align_bytes=64) for h in range(2)]
@@ -88,7 +94,7 @@ def tile_list_thermometer_kernel(tc, xt_words, xt_scales, w_words, w_scales, sg,
             nc.tensor.matmul_mx(
                 out=acc[:],
                 lhsT=w_codes[:].bitcast(U8).bitcast(FP4X4),
-                lhsT_scale=ws_plane[:].bitcast(U8),
+                lhsT_scale=ws_plane[:, 0, :].bitcast(U8),
                 rhs=g_words[h][:].bitcast(FP8X4),
                 rhs_scale=g_scales[h][:],
                 start=True,

@@ -15,7 +15,7 @@ ACT = mybir.ActivationFunctionType
 K, T, J, Q, R, O, N, E = 512, 1024, 256, 128, 512, 128, 256, 256
 P = 128
 QUADS = 4
-HEAD = 448
+HEAD = 496
 FLOPS = 2 * K * Q * J + 2 * R * N * O
 
 
@@ -101,8 +101,8 @@ def tile_list_thermometer_kernel(tc, xt_words, xt_scales, w_words, w_scales, sg,
                 stop=True,
             )
             a_ps.append(acc)
-        nc.scalar.copy(a_sb[:, 0:half], a_ps[0][:])
-        nc.vector.tensor_copy(a_sb[:, half:J], a_ps[1][:])
+        nc.vector.tensor_copy(a_sb[:, 0:half], a_ps[0][:])
+        nc.scalar.copy(a_sb[:, half:J], a_ps[1][:])
 
         hid = sb.tile([P, 4 * O], BF16, name="hid", align_bytes=64)
         for i in range(4):
@@ -124,6 +124,9 @@ def tile_list_thermometer_kernel(tc, xt_words, xt_scales, w_words, w_scales, sg,
                 stop=True,
             )
             p_sb = sb.tile([P, O], F32, name="p_sb%d" % h)
-            nc.vector.tensor_copy(p_sb[:], p_ps[:])
+            if h == 0:
+                nc.scalar.copy(p_sb[:], p_ps[:])
+            else:
+                nc.vector.tensor_copy(p_sb[:], p_ps[:])
             nc.scalar.activation(page[h][:].indirect(list3[:]), p_sb[:], ACT.Copy, scale=gain[:, h : h + 1])
             nc.sync.dma_start(out[P * h : P * (h + 1), :], page[h][:])

from contextlib import ExitStack

import concourse.mybir as mybir

F32 = mybir.dt.float32
BF16 = mybir.dt.bfloat16
I32 = mybir.dt.int32
U32 = mybir.dt.uint32
U16 = mybir.dt.uint16
U8 = mybir.dt.uint8
FP8X4 = mybir.dt.float8_e4m3fn_x4
FP4X4 = mybir.dt.float4_e2m1fn_x4
ACT = mybir.ActivationFunctionType

K, T, J, Q, R, O, N, E = 512, 1024, 256, 128, 512, 128, 256, 256
P = 128
QUADS = 4
HEAD = 496
FLOPS = 2 * K * Q * J + 2 * R * N * O


def tile_list_thermometer_kernel(tc, xt_words, xt_scales, w_words, w_scales, sg, ba, bb, bc, bd,
                                    wb_words, wb_scales, so, offs, offs2, offs3, out):
    nc = tc.nc
    with ExitStack() as ctx:
        sb = ctx.enter_context(tc.tile_pool(name="sb", bufs=1))
        ps = ctx.enter_context(tc.psum_pool(name="ps", bufs=1))
        ctx.enter_context(nc.allow_non_contiguous_dma(reason="one float32 value a partition"))

        xs_plane = sb.tile([P, T // 4], I32, name="xs_plane", align_bytes=64)
        nc.vector.memset(xs_plane[:], 0)
        ws_plane = sb.tile([P, 2, Q // 4], I32, name="ws_plane", align_bytes=64)
        nc.vector.memset(ws_plane[:], 0)
        wbs_plane = sb.tile([P, N // 4], I32, name="wbs_plane", align_bytes=64)
        nc.vector.memset(wbs_plane[:], 0)

        ws_rows = sb.tile([4, QUADS, Q // 4], I32, name="ws_rows")
        nc.scalar.dma_start(ws_rows[:], w_scales[0].bitcast(I32).rearrange("(q r) c -> r q c", r=4))
        x_words = sb.tile([P, T], I32, name="x_words", align_bytes=64)
        x_src = xt_words[0].rearrange("p c r -> p (c r)").bitcast(I32)
        nc.scalar.dma_start(x_words[:, 0:HEAD], x_src[:, 0:HEAD])
        for q in (2, 3):
            nc.scalar.dma_start(xs_plane[32 * q : 32 * q + 4, :], xt_scales[0].bitcast(I32)[4 * q : 4 * q + 4, :])

        warm = sb.tile([P, 1], F32, name="warm")
        nc.vector.memset(warm[:], 0.0)
        warm_out = sb.tile([P, 1], F32, name="warm_out")
        nc.scalar.activation(warm_out[:], warm[:], ACT.Sigmoid)

        list1 = sb.tile([P, J // 16], U16, name="list1")
        nc.sync.dma_start(list1[:], offs)
        for q in (0, 1):
            nc.sync.dma_start(xs_plane[32 * q : 32 * q + 4, :], xt_scales[0].bitcast(I32)[4 * q : 4 * q + 4, :])
        nc.sync.dma_start(x_words[:, HEAD:T], x_src[:, HEAD:T])
        w_codes = sb.tile([P, Q // 2], I32, name="w_codes", align_bytes=64)
        nc.sync.dma_start(w_codes[:], w_words[0].bitcast(I32))

        list2 = sb.tile([P, O // 16], U16, name="list2")
        nc.sync.dma_start(list2[:], offs2)
        bias = [sb.tile([P, 1], F32, name="bias%d" % i) for i in range(4)]
        for i, src in enumerate((ba, bb, bc, bd)):
            nc.sync.dma_start(bias[i][:], src)
        for q in range(QUADS):
            nc.sync.dma_start(wbs_plane[32 * q : 32 * q + 4, :], wb_scales[0].bitcast(I32)[4 * q : 4 * q + 4, :])
        list3 = sb.tile([P, O // 16], U16, name="list3")
        nc.sync.dma_start(list3[:], offs3)

        slope = sb.tile([P, 1], F32, name="slope")
        nc.gpsimd.dma_start(slope[:], sg)
        wb_codes = sb.tile([P, N // 2], I32, name="wb_codes", align_bytes=64)
        nc.gpsimd.dma_start(wb_codes[:], wb_words[0].bitcast(I32))
        gain = sb.tile([P, 2], F32, name="gain")
        nc.gpsimd.dma_start(gain[:], so.rearrange("(h p) o -> p (h o)", p=P))

        page = [sb.tile([P, E], F32, name="page%d" % h) for h in range(2)]
        for h in range(2):
            nc.vector.memset(page[h][:], 0.0)

        for q in range(2):
            nc.vector.tensor_copy(ws_plane[32 * q : 32 * q + 4, :, :], ws_rows[:, q:QUADS:2, :])
        nc.vector.tensor_copy(ws_plane[64:128, 0, :], ws_plane[0:64, 1, :])

        half = J // 2
        g_scales = [sb.tile([P, half], U8, name="g_scales%d" % h, align_bytes=64) for h in range(2)]
        g_words = [sb.tile([P, half], U32, name="g_words%d" % h, align_bytes=64) for h in range(2)]
        part = [list1[:, h * (half // 16) : (h + 1) * (half // 16)] for h in range(2)]
        for h in range(2):
            nc.vector.tensor_copy(g_scales[h][:], xs_plane[:].bitcast(U8).indirect(part[h]))
        a_sb = sb.tile([P, J], F32, name="a_sb")
        a_ps = []
        for h in range(2):
            nc.vector.tensor_copy(g_words[h][:], x_words[:].bitcast(U32).indirect(part[h]))
            acc = ps.tile([P, half], F32, name="a_ps%d" % h)
            nc.tensor.matmul_mx(
                out=acc[:],
                lhsT=w_codes[:].bitcast(U8).bitcast(FP4X4),
                lhsT_scale=ws_plane[:, 0, :].bitcast(U8),
                rhs=g_words[h][:].bitcast(FP8X4),
                rhs_scale=g_scales[h][:],
                start=True,
                stop=True,
            )
            a_ps.append(acc)
        nc.vector.tensor_copy(a_sb[:, 0:half], a_ps[0][:])
        nc.scalar.copy(a_sb[:, half:J], a_ps[1][:])

        hid = sb.tile([P, 4 * O], BF16, name="hid", align_bytes=64)
        for i in range(4):
            nc.scalar.activation(hid[:, i : 4 * O : 4], a_sb[:].indirect(list2[:]), ACT.Sigmoid, bias=bias[i][:], scale=slope[:])

        h_codes = sb.tile([P, O], U32, name="h_codes", align_bytes=64)
        h_scales = sb.tile([P, O], U8, name="h_scales", align_bytes=64)
        nc.vector.quantize_mx(out=h_codes[:].bitcast(FP8X4), scales=h_scales[:], in_=hid[:])

        for h in range(2):
            p_ps = ps.tile([P, O], F32, name="p_ps%d" % h)
            nc.tensor.matmul_mx(
                out=p_ps[:],
                lhsT=wb_codes[:].bitcast(U8)[:, 2 * P * h : 2 * P * (h + 1)].bitcast(FP4X4),
                lhsT_scale=wbs_plane[:].bitcast(U8)[:, P * h : P * (h + 1)],
                rhs=h_codes[:].bitcast(FP8X4),
                rhs_scale=h_scales[:],
                start=True,
                stop=True,
            )
            p_sb = sb.tile([P, O], F32, name="p_sb%d" % h)
            if h == 0:
                nc.scalar.copy(p_sb[:], p_ps[:])
            else:
                nc.vector.tensor_copy(p_sb[:], p_ps[:])
            nc.scalar.activation(page[h][:].indirect(list3[:]), p_sb[:], ACT.Copy, scale=gain[:, h : h + 1])
            nc.sync.dma_start(out[P * h : P * (h + 1), :], page[h][:])
